import numpy as np
import ml_dtypes


def mxq(x, axis, fmt="e4m3"):
    dtype, down = {"e4m3": (ml_dtypes.float8_e4m3fn, 7), "e5m2": (ml_dtypes.float8_e5m2, 14)}[fmt]
    v = np.moveaxis(np.asarray(x, np.float32).astype(ml_dtypes.bfloat16).astype(np.float64), axis, -1)
    blocks = v.reshape(v.shape[:-1] + (-1, 32))
    amax = np.abs(blocks).max(-1, keepdims=True)
    byte = np.maximum(np.where(amax > 0, np.frexp(amax)[1] - 1 + 127, 0) - down, 1)
    scale = np.exp2(byte - 127.0)
    codes = (blocks / scale).astype(np.float32).astype(dtype).astype(np.float64)
    return np.moveaxis((codes * scale).reshape(v.shape), -1, axis)


WIDE = False


def mx_kscale(k):
    if not WIDE:
        return np.ones(k)
    levels = np.array([10, -10, 5, -5, 0])
    if k % 512:
        return np.exp2(np.random.permutation(np.resize(levels, k // 32))).repeat(32)
    a = np.empty((k // 512, 16))
    for p in range(k // 512):
        a[p, :8] = np.random.permutation(np.resize(levels, 8))
        for g in range(8):
            far = levels[np.abs(levels - a[p, g]) >= 10]
            a[p, g + 8] = far[np.random.randint(len(far))]
    return np.exp2(a.ravel()).repeat(32)


def f64(x):
    return np.asarray(x).astype(np.float64)


def striped(idx):
    return np.tile(idx.reshape(-1, 16).T, (8, 1)).astype(np.uint16)


def unstriped(offs):
    return offs[:16].T.reshape(-1).astype(np.int64)


E2M1 = np.array([0.0, 0.5, 1.0, 1.5, 2.0, 3.0, 4.0, 6.0, -0.0, -0.5, -1.0, -1.5, -2.0, -3.0, -4.0, -6.0])


def pack_weight(w, fmt):
    k, n = w.shape
    w = f64(np.asarray(w, np.float32).astype(ml_dtypes.bfloat16)).reshape(k // 32, 32, n)
    amax = np.abs(w).max(1)
    if fmt == "e4m3":
        byte = np.frexp(amax)[1] - 1 + 127 - 7
    else:
        mant, ex = np.frexp(amax / 6.0)
        byte = np.where(mant > 0.5, ex, ex - 1) + 127
    byte = np.clip(np.where(amax > 0, byte, 1), 1, 254)
    scaled = (w * np.exp2(127.0 - byte)[:, None, :]).reshape(k, n).astype(np.float32)
    by_word = np.ascontiguousarray(scaled.reshape(k // 512, 128, 4, n).transpose(0, 1, 3, 2))
    if fmt == "e4m3":
        words = by_word.astype(ml_dtypes.float8_e4m3fn).view(np.uint8)
    else:
        c = by_word.astype(ml_dtypes.float4_e2m1fn).view(np.uint8) & 0xF
        words = (c[..., 0::2] | (c[..., 1::2] << 4)).reshape(k // 512, 128, 2 * n)
    return np.ascontiguousarray(words), np.ascontiguousarray(byte.astype(np.uint8).reshape(k // 512, 16, n))


def unpack_weight(words, scales, fmt):
    g, _, n = scales.shape
    words = np.ascontiguousarray(words).reshape(g, 128, n, -1)
    if fmt == "e4m3":
        vals = words.view(ml_dtypes.float8_e4m3fn).astype(np.float64)
    else:
        nib = np.empty((g, 128, n, 4), np.uint8)
        nib[..., 0::2] = words & 0xF
        nib[..., 1::2] = words >> 4
        vals = E2M1[nib]
    vals = vals * np.repeat(np.exp2(scales.astype(np.float64) - 127.0), 8, axis=1)[..., None]
    return vals.transpose(0, 1, 3, 2).reshape(g * 512, n)


def gelu(v):
    return 0.5 * v * (1.0 + np.tanh(np.sqrt(2.0 / np.pi) * (v + 0.044715 * v**3)))


K, H, N, T, S, P1, P2, P3 = 512, 1024, 512, 4096, 2048, 1024, 512, 256

def setup_inputs():
    n = np.random.standard_normal
    s = mx_kscale(K)[:, None]
    u = mx_kscale(H)[:, None]
    tab_words, tab_scales = pack_weight(n((K, T)) * s, "e4m3")
    w4_words, w4_scales = pack_weight(1.5 * n((K, H)) / np.sqrt(K) / s, "e2m1")
    views = np.random.permutation(S)
    vegs = np.random.permutation(P1)
    growers = np.random.permutation(P2)
    return {
        "tab_words": tab_words, "tab_scales": tab_scales,
        "offs": striped(np.random.permutation(T)[:S]),
        "pos1": striped(views[:P1]), "pos2": striped(views[P1:]),
        "pos3": striped(vegs[:P2]), "pos4": striped(vegs[P2:]),
        "pos5": striped(growers[:P3]), "pos6": striped(growers[P3:]),
        "w4_words": w4_words, "w4_scales": w4_scales,
        "d": (0.8 * n(P2)).astype(np.float32),
        "gain": (np.exp(0.3 * n(H)) * u[:, 0]).astype(np.float32),
        "w2": (0.6 * n((H, N)) / np.sqrt(H) / u).astype(np.float32),
    }

def reference(tab_words, tab_scales, offs, pos1, pos2, pos3, pos4, pos5, pos6,
              w4_words, w4_scales, d, gain, w2):
    v = unpack_weight(tab_words, tab_scales, "e4m3")[:, unstriped(offs)]
    w4 = unpack_weight(w4_words, w4_scales, "e2m1")
    c = w4.T @ v
    h = c / (1.0 + np.exp(-c))
    a1 = np.maximum(h[:, unstriped(pos1)], h[:, unstriped(pos2)])
    a2 = a1[:, unstriped(pos3)] * a1[:, unstriped(pos4)] + f64(d)[None, :]
    a3 = (a2[:, unstriped(pos5)] - a2[:, unstriped(pos6)]) * f64(gain)[:, None]
    y = mxq(f64(w2), 0, "e4m3").T @ mxq(a3, 0, "e4m3")
    return np.tanh(y)

@@ -1,0 +1,184 @@
+from contextlib import ExitStack
+
+import concourse.mybir as mybir
+
+K, H, N, T, S, P1, P2, P3 = 512, 1024, 512, 4096, 2048, 1024, 512, 256
+FLOPS = 2 * K * H * S + 2 * H * N * P3
+
+F32 = mybir.dt.float32
+BF16 = mybir.dt.bfloat16
+I32 = mybir.dt.int32
+U32 = mybir.dt.uint32
+U16 = mybir.dt.uint16
+U8 = mybir.dt.uint8
+FP8X4 = mybir.dt.float8_e4m3fn_x4
+FP4X4 = mybir.dt.float4_e2m1fn_x4
+ALU = mybir.AluOpType
+ACT = mybir.ActivationFunctionType
+
+P = 128
+PACK = 4
+K_PASS = P * PACK
+PASSES = H // K_PASS
+SLICES = H // P
+BANK = 512
+
+
+def load_scale_rows(queue, plane, rows):
+    for q in range(4):
+        queue.dma_start(out=plane[32 * q : 32 * q + 4, :].bitcast(I32), in_=rows[4 * q : 4 * q + 4, :].bitcast(I32))
+
+
+def tile_list_vegetable_class_judging_kernel(
+    tc, tab_words, tab_scales, offs, pos1, pos2, pos3, pos4, pos5, pos6, w4_words, w4_scales, d, gain, w2, out
+):
+    nc = tc.nc
+    with ExitStack() as ctx:
+        keep = ctx.enter_context(tc.tile_pool(name="keep", bufs=1))
+        work = ctx.enter_context(tc.tile_pool(name="work", bufs=2))
+        psum = ctx.enter_context(tc.psum_pool(name="psum", bufs=4))
+
+        def load_list(src, name):
+            tile = keep.tile(list(src.shape), U16, name=name)
+            nc.sync.dma_start(tile[:], src)
+            return tile
+
+        idx, p1, p2, p3 = [load_list(src, name) for src, name in ((offs, "idx"), (pos1, "p1"), (pos2, "p2"), (pos3, "p3"))]
+        tab_w = keep.tile([P, T], U32, align_bytes=64, tag="tab_w")
+        nc.sync.dma_start(out=tab_w[:].bitcast(I32), in_=tab_words[0].rearrange("p t i -> p (t i)").bitcast(I32))
+        p4, p5, p6 = [load_list(src, name) for src, name in ((pos4, "p4"), (pos5, "p5"), (pos6, "p6"))]
+        tab_s = keep.tile([P, T], U8, align_bytes=64, tag="tab_s")
+        nc.vector.memset(tab_s[:].bitcast(I32), 0)
+        load_scale_rows(nc.scalar, tab_s, tab_scales[0])
+
+        w4_raw = keep.tile([P, 2 * H], U8, align_bytes=64, tag="w4_raw")
+        nc.gpsimd.dma_start(out=w4_raw[:].bitcast(I32), in_=w4_words[0].bitcast(I32))
+        w4s_raw = keep.tile([P, H], U8, align_bytes=64)
+        nc.vector.memset(w4s_raw[:].bitcast(I32), 0)
+        load_scale_rows(nc.scalar, w4s_raw, w4_scales[0])
+        gain_col = keep.tile([P, PASSES, PACK], F32)
+        nc.gpsimd.dma_start(out=gain_col[:], in_=gain.rearrange("(b p t) -> p b t", b=PASSES, t=PACK))
+
+        v_s = []
+        for c in range(S // BANK):
+            scales = keep.tile([P, BANK], U8, align_bytes=64, name="v_s%d" % c)
+            nc.vector.tensor_copy(scales[:], tab_s[:].indirect(idx[:, c * BANK // 16 : (c + 1) * BANK // 16]))
+            v_s.append(scales)
+
+        w4_c = keep.tile([P, SLICES, 2 * P], U8, align_bytes=64)
+        nc.vector.tensor_copy(
+            out=w4_c[:].bitcast(U16).rearrange("p (b t) m -> p b t m", t=PACK),
+            in_=w4_raw[:].bitcast(U16).rearrange("p (b m t) -> p b t m", b=PASSES, t=PACK),
+        )
+        w4_s = keep.tile([P, SLICES, P], U8, align_bytes=64)
+        nc.vector.tensor_copy(
+            out=w4_s[:].rearrange("p (b t) m -> p b t m", t=PACK),
+            in_=w4s_raw[:].rearrange("p (b m t) -> p b t m", b=PASSES, t=PACK),
+        )
+
+        v_w = []
+        for c in range(S // BANK):
+            words = keep.tile([P, BANK], U32, align_bytes=64, name="v_w%d" % c)
+            nc.vector.tensor_copy(words[:], tab_w[:].indirect(idx[:, c * BANK // 16 : (c + 1) * BANK // 16]))
+            v_w.append(words)
+
+        w2_raw = []
+        for b, tag in enumerate(("w4_raw", "tab_w")):
+            raw = keep.tile([P, PACK, N], F32, align_bytes=64, name="w2_raw%d" % b, tag=tag)
+            nc.sync.dma_start(out=raw[:], in_=w2[b * K_PASS : (b + 1) * K_PASS, :].rearrange("(p t) n -> p t n", t=PACK))
+            w2_raw.append(raw)
+        d_row = keep.tile([P, P2], F32, align_bytes=64, tag="tab_s")
+        nc.sync.dma_start(out=d_row[:], in_=d.partition_broadcast(P))
+        w2_c = keep.tile([P, PASSES, N], U32, align_bytes=64)
+        w2_s = keep.tile([P, PASSES, N], U8, align_bytes=64)
+
+        def quantize_w2(b):
+            grouped = keep.tile([P, N, PACK], BF16, align_bytes=64, name="w2_bf%d" % b)
+            nc.scalar.copy(
+                out=grouped[:].rearrange("p (c i) t -> p c t i", i=4),
+                in_=w2_raw[b][:].rearrange("p t (c i) -> p c t i", i=4),
+            )
+            nc.vector.quantize_mx(
+                out=w2_c[:, b, :].bitcast(FP8X4), scales=w2_s[:, b, :], in_=grouped[:].rearrange("p n t -> p (n t)")
+            )
+
+        a3_bf = [keep.tile([P, P3, PACK], BF16, align_bytes=64, name="a3_bf%d" % b) for b in range(PASSES)]
+        a3_c = [keep.tile([P, P3], U32, align_bytes=64, name="a3_c%d" % b) for b in range(PASSES)]
+        a3_s = [keep.tile([P, P3], U8, align_bytes=64, name="a3_s%d" % b) for b in range(PASSES)]
+        h, a1, a2 = {}, {}, {}
+
+        def features(s):
+            h[s] = work.tile([P, S], F32, name="h", bufs=3)
+            for c in range(S // BANK):
+                cols = slice(c * BANK, (c + 1) * BANK)
+                acc = psum.tile([P, BANK], F32, name="acc")
+                nc.tensor.matmul_mx(
+                    out=acc[:],
+                    lhsT=w4_c[:, s, :].bitcast(FP4X4),
+                    lhsT_scale=w4_s[:, s, :],
+                    rhs=v_w[c][:].bitcast(FP8X4),
+                    rhs_scale=v_s[c][:],
+                    start=True,
+                    stop=True,
+                )
+                nc.scalar.activation(out=h[s][:, cols], in_=acc[:], func=ACT.Silu)
+
+        def level1(s):
+            view1 = work.tile([P, P1], F32, name="view1")
+            view2 = work.tile([P, P1], F32, name="view2")
+            nc.vector.tensor_copy(view1[:], h[s][:].indirect(p1[:]))
+            nc.vector.tensor_copy(view2[:], h[s][:].indirect(p2[:]))
+            a1[s] = work.tile([P, P1], F32, name="a1")
+            nc.vector.tensor_tensor(a1[s][:], view1[:], view2[:], ALU.max)
+
+        def level2(s):
+            veg = work.tile([P, P2], F32, name="veg")
+            nc.vector.tensor_copy(veg[:], a1[s][:].indirect(p3[:]))
+            prod = work.tile([P, P2], F32, name="prod")
+            nc.vector.tensor_tensor(prod[:], a1[s][:].indirect(p4[:]), veg[:], ALU.mult)
+            a2[s] = work.tile([P, P2], F32, name="a2")
+            nc.vector.tensor_tensor(a2[s][:], prod[:], d_row[:], ALU.add)
+
+        def level3(s):
+            b, t = divmod(s, PACK)
+            other = work.tile([P, P3], F32, name="other")
+            nc.vector.tensor_copy(other[:], a2[s][:].indirect(p6[:]))
+            diff = work.tile([P, P3], F32, name="diff")
+            nc.vector.tensor_tensor(diff[:], a2[s][:].indirect(p5[:]), other[:], ALU.subtract)
+            nc.scalar.activation(out=a3_bf[b][:, :, t], in_=diff[:], func=ACT.Copy, scale=gain_col[:, b, t : t + 1])
+            if t == PACK - 1:
+                nc.vector.quantize_mx(
+                    out=a3_c[b][:].bitcast(FP8X4), scales=a3_s[b][:], in_=a3_bf[b][:].rearrange("p j t -> p (j t)")
+                )
+
+        for step in range(SLICES + 3):
+            if step < SLICES:
+                features(step)
+            if step in (1, 3):
+                quantize_w2(step // 2)
+            if 0 <= step - 1 < SLICES:
+                level1(step - 1)
+            if 0 <= step - 2 < SLICES:
+                level2(step - 2)
+            if 0 <= step - 3 < SLICES:
+                level3(step - 3)
+
+        halves = out.rearrange("(u e p) j -> u p e j", e=2, p=P)
+        accs = [psum.tile([P, 2, P3], F32, name="acc") for u in range(2)]
+        for b in range(PASSES):
+            for u in range(2):
+                for e in range(2):
+                    cols = slice((2 * u + e) * P, (2 * u + e + 1) * P)
+                    nc.tensor.matmul_mx(
+                        out=accs[u][:, e, :],
+                        lhsT=w2_c[:, b, cols].bitcast(FP8X4),
+                        lhsT_scale=w2_s[:, b, cols],
+                        rhs=a3_c[b][:].bitcast(FP8X4),
+                        rhs_scale=a3_s[b][:],
+                        start=(b == 0 and e == 0),
+                        stop=(b == PASSES - 1 and e == 1),
+                    )
+        for u in range(2):
+            res = work.tile([P, 2, P3], F32, name="res")
+            nc.scalar.activation(out=res[:], in_=accs[u][:], func=ACT.Tanh)
+            nc.sync.dma_start(out=halves[u], in_=res[:])

@@ -1,6 +1,7 @@
 from contextlib import ExitStack
 
 import concourse.mybir as mybir
+from concourse.masks import make_identity
 
 K, H, N, T, S, P1, P2, P3 = 512, 1024, 512, 4096, 2048, 1024, 512, 256
 FLOPS = 2 * K * H * S + 2 * H * N * P3
@@ -22,6 +23,7 @@ K_PASS = P * PACK
 PASSES = H // K_PASS
 SLICES = H // P
 BANK = 512
+MOVED = 512
 
 
 def load_scale_rows(queue, plane, rows):
@@ -36,34 +38,33 @@ def tile_list_vegetable_class_judging_kernel(
     with ExitStack() as ctx:
         keep = ctx.enter_context(tc.tile_pool(name="keep", bufs=1))
         work = ctx.enter_context(tc.tile_pool(name="work", bufs=2))
-        psum = ctx.enter_context(tc.psum_pool(name="psum", bufs=4))
+        psum = ctx.enter_context(tc.psum_pool(name="psum", bufs=2))
 
         def load_list(src, name):
             tile = keep.tile(list(src.shape), U16, name=name)
             nc.sync.dma_start(tile[:], src)
             return tile
 
-        idx, p1, p2, p3 = [load_list(src, name) for src, name in ((offs, "idx"), (pos1, "p1"), (pos2, "p2"), (pos3, "p3"))]
         tab_w = keep.tile([P, T], U32, align_bytes=64, tag="tab_w")
         nc.sync.dma_start(out=tab_w[:].bitcast(I32), in_=tab_words[0].rearrange("p t i -> p (t i)").bitcast(I32))
+        idx, p1, p2, p3 = [load_list(src, name) for src, name in ((offs, "idx"), (pos1, "p1"), (pos2, "p2"), (pos3, "p3"))]
         p4, p5, p6 = [load_list(src, name) for src, name in ((pos4, "p4"), (pos5, "p5"), (pos6, "p6"))]
-        tab_s = keep.tile([P, T], U8, align_bytes=64, tag="tab_s")
-        nc.vector.memset(tab_s[:].bitcast(I32), 0)
-        load_scale_rows(nc.scalar, tab_s, tab_scales[0])
 
         w4_raw = keep.tile([P, 2 * H], U8, align_bytes=64, tag="w4_raw")
         nc.gpsimd.dma_start(out=w4_raw[:].bitcast(I32), in_=w4_words[0].bitcast(I32))
         w4s_raw = keep.tile([P, H], U8, align_bytes=64)
         nc.vector.memset(w4s_raw[:].bitcast(I32), 0)
+        tab_s = keep.tile([P, T], U8, align_bytes=64, tag="tab_s")
+        nc.vector.memset(tab_s[:].bitcast(I32), 0)
         load_scale_rows(nc.scalar, w4s_raw, w4_scales[0])
+        load_scale_rows(nc.scalar, tab_s, tab_scales[0])
+        ident = keep.tile([P, P], F32)
+        make_identity(nc, ident[:])
         gain_col = keep.tile([P, PASSES, PACK], F32)
         nc.gpsimd.dma_start(out=gain_col[:], in_=gain.rearrange("(b p t) -> p b t", b=PASSES, t=PACK))
-
-        v_s = []
-        for c in range(S // BANK):
-            scales = keep.tile([P, BANK], U8, align_bytes=64, name="v_s%d" % c)
-            nc.vector.tensor_copy(scales[:], tab_s[:].indirect(idx[:, c * BANK // 16 : (c + 1) * BANK // 16]))
-            v_s.append(scales)
+        d_col = keep.tile([P, P2 // P], F32)
+        with nc.allow_non_contiguous_dma(reason="one value of d for each partition"):
+            nc.gpsimd.dma_start(out=d_col[:], in_=d.rearrange("(c p) -> p c", p=P))
 
         w4_c = keep.tile([P, SLICES, 2 * P], U8, align_bytes=64)
         nc.vector.tensor_copy(
@@ -81,6 +82,12 @@ def tile_list_vegetable_class_judging_kernel(
             words = keep.tile([P, BANK], U32, align_bytes=64, name="v_w%d" % c)
             nc.vector.tensor_copy(words[:], tab_w[:].indirect(idx[:, c * BANK // 16 : (c + 1) * BANK // 16]))
             v_w.append(words)
+
+        v_s = []
+        for c in range(S // BANK):
+            scales = keep.tile([P, BANK], U8, align_bytes=64, name="v_s%d" % c)
+            nc.vector.tensor_copy(scales[:], tab_s[:].indirect(idx[:, c * BANK // 16 : (c + 1) * BANK // 16]))
+            v_s.append(scales)
 
         w2_raw = []
         for b, tag in enumerate(("w4_raw", "tab_w")):
@@ -102,16 +109,22 @@ def tile_list_vegetable_class_judging_kernel(
                 out=w2_c[:, b, :].bitcast(FP8X4), scales=w2_s[:, b, :], in_=grouped[:].rearrange("p n t -> p (n t)")
             )
 
-        a3_bf = [keep.tile([P, P3, PACK], BF16, align_bytes=64, name="a3_bf%d" % b) for b in range(PASSES)]
-        a3_c = [keep.tile([P, P3], U32, align_bytes=64, name="a3_c%d" % b) for b in range(PASSES)]
-        a3_s = [keep.tile([P, P3], U8, align_bytes=64, name="a3_s%d" % b) for b in range(PASSES)]
+        def per_half(shape, dtype, name):
+            return [
+                [keep.tile(shape, dtype, align_bytes=64, name="%s%d%d" % (name, b, u)) for u in range(2)]
+                for b in range(PASSES)
+            ]
+
+        a3_bf = per_half([P, P3 // 2, PACK], BF16, "a3_bf")
+        a3_c = per_half([P, P3 // 2], U32, "a3_c")
+        a3_s = per_half([P, P3 // 2], U8, "a3_s")
         h, a1, a2 = {}, {}, {}
 
         def features(s):
-            h[s] = work.tile([P, S], F32, name="h", bufs=3)
+            h[s] = work.tile([P, S], F32, name="h", bufs=2)
             for c in range(S // BANK):
                 cols = slice(c * BANK, (c + 1) * BANK)
-                acc = psum.tile([P, BANK], F32, name="acc")
+                acc = psum.tile([P, BANK], F32, name="acc", bufs=4)
                 nc.tensor.matmul_mx(
                     out=acc[:],
                     lhsT=w4_c[:, s, :].bitcast(FP4X4),
@@ -123,62 +136,119 @@ def tile_list_vegetable_class_judging_kernel(
                 )
                 nc.scalar.activation(out=h[s][:, cols], in_=acc[:], func=ACT.Silu)
 
+        def turned(terms, name):
+            bank = psum.tile([P, BANK], F32, name=name)
+            count = BANK // P * len(terms)
+            n = 0
+            for blk in range(BANK // P):
+                cols = slice(blk * P, (blk + 1) * P)
+                for term in terms:
+                    nc.tensor.matmul(
+                        bank[:, cols], term[:, cols], ident[:], is_transpose=True, start=(n == 0), stop=(n == count - 1)
+                    )
+                    n += 1
+            return bank
+
+        scratch = keep.tile([P, BANK], F32)
+        last = SLICES - 1
+
+        def halves(width):
+            half = width // 2
+            return [(slice(u * half, (u + 1) * half), slice(u * half // 16, (u + 1) * half // 16)) for u in range(2)]
+
+        (moved, moved_entries), (kept, kept_entries) = halves(P1)
+
+        veg, other = {}, {}
+
         def level1(s):
-            view1 = work.tile([P, P1], F32, name="view1")
-            view2 = work.tile([P, P1], F32, name="view2")
-            nc.vector.tensor_copy(view1[:], h[s][:].indirect(p1[:]))
-            nc.vector.tensor_copy(view2[:], h[s][:].indirect(p2[:]))
-            a1[s] = work.tile([P, P1], F32, name="a1")
-            nc.vector.tensor_tensor(a1[s][:], view1[:], view2[:], ALU.max)
+            window = h[s][:]
+            a1[s] = work.tile([P, P1], F32, name="a1", bufs=4)
+            first = work.tile([P, P1], F32, name="first", bufs=3)
+            nc.vector.tensor_copy(first[:], window.indirect(p1[:]))
+            nc.vector.tensor_copy(scratch[:], window.indirect(p2[:, kept_entries]))
+            gap = work.tile([P, BANK], F32, name="gap", bufs=3)
+            nc.vector.tensor_tensor(gap[:], window.indirect(p2[:, moved_entries]), first[:, moved], ALU.subtract)
+            nc.vector.tensor_tensor(a1[s][:, kept], first[:, kept], scratch[:], ALU.max)
+            rise = work.tile([P, BANK], F32, name="rise")
+            nc.scalar.activation(out=rise[:], in_=gap[:], func=ACT.Relu)
+            bank = turned([first, rise], "there")
+            across = work.tile([P, BANK], F32, name="across", bufs=3)
+            nc.scalar.copy(out=across[:], in_=bank[:])
+            bank = turned([across], "back")
+            nc.scalar.copy(out=a1[s][:, moved], in_=bank[:])
 
-        def level2(s):
-            veg = work.tile([P, P2], F32, name="veg")
-            nc.vector.tensor_copy(veg[:], a1[s][:].indirect(p3[:]))
+        def first_vegs(s):
+            nc.vector.tensor_copy(scratch[:], a1[s][:].indirect(p3[:]))
+
+        def products(s):
             prod = work.tile([P, P2], F32, name="prod")
-            nc.vector.tensor_tensor(prod[:], a1[s][:].indirect(p4[:]), veg[:], ALU.mult)
-            a2[s] = work.tile([P, P2], F32, name="a2")
-            nc.vector.tensor_tensor(a2[s][:], prod[:], d_row[:], ALU.add)
+            nc.vector.tensor_tensor(prod[:], a1[s][:].indirect(p4[:]), scratch[:], ALU.mult)
+            a2[s] = work.tile([P, P2], F32, name="a2", bufs=4)
+            if s == last:
+                nc.vector.tensor_tensor(a2[s][:], prod[:], d_row[:], ALU.add)
+                return
+            bank = turned([prod], "there")
+            across = work.tile([P, BANK], F32, name="across", bufs=3)
+            for blk in range(P2 // P):
+                cols = slice(blk * P, (blk + 1) * P)
+                nc.scalar.activation(
+                    out=across[:, cols], in_=bank[:, cols], func=ACT.Identity, bias=d_col[:, blk : blk + 1]
+                )
+            bank = turned([across], "back")
+            nc.scalar.copy(out=a2[s][:], in_=bank[:])
 
-        def level3(s):
+        def second_growers(s):
+            other[s] = h[min(s + 4, last)][:, :P3]
+            nc.vector.tensor_copy(other[s], a2[s][:].indirect(p6[:]))
+
+        def differences(s):
             b, t = divmod(s, PACK)
-            other = work.tile([P, P3], F32, name="other")
-            nc.vector.tensor_copy(other[:], a2[s][:].indirect(p6[:]))
-            diff = work.tile([P, P3], F32, name="diff")
-            nc.vector.tensor_tensor(diff[:], a2[s][:].indirect(p5[:]), other[:], ALU.subtract)
-            nc.scalar.activation(out=a3_bf[b][:, :, t], in_=diff[:], func=ACT.Copy, scale=gain_col[:, b, t : t + 1])
-            if t == PACK - 1:
-                nc.vector.quantize_mx(
-                    out=a3_c[b][:].bitcast(FP8X4), scales=a3_s[b][:], in_=a3_bf[b][:].rearrange("p j t -> p (j t)")
+            parts = halves(P3) if s == last else [(slice(0, P3), slice(0, P3 // 16))]
+            diff = work.tile([P, P3], F32, name="diff", bufs=3)
+            for cols, entries in parts:
+                nc.vector.tensor_tensor(diff[:, cols], a2[s][:].indirect(p5[:, entries]), other[s][:, cols], ALU.subtract)
+            for u, (cols, entries) in enumerate(halves(P3)):
+                nc.scalar.activation(
+                    out=a3_bf[b][u][:, :, t], in_=diff[:, cols], func=ACT.Copy, scale=gain_col[:, b, t : t + 1]
                 )
 
-        for step in range(SLICES + 3):
-            if step < SLICES:
-                features(step)
-            if step in (1, 3):
-                quantize_w2(step // 2)
-            if 0 <= step - 1 < SLICES:
-                level1(step - 1)
-            if 0 <= step - 2 < SLICES:
-                level2(step - 2)
-            if 0 <= step - 3 < SLICES:
-                level3(step - 3)
+        def quantize_a3(b):
+            for u in range(2):
+                nc.vector.quantize_mx(
+                    out=a3_c[b][u][:].bitcast(FP8X4),
+                    scales=a3_s[b][u][:],
+                    in_=a3_bf[b][u][:].rearrange("p j t -> p (j t)"),
+                )
 
-        halves = out.rearrange("(u e p) j -> u p e j", e=2, p=P)
-        accs = [psum.tile([P, 2, P3], F32, name="acc") for u in range(2)]
+        features(0)
+        quantize_w2(0)
+        order = ((features, -1), (level1, 0), (second_growers, 4), (first_vegs, 2), (differences, 4), (products, 2))
+        for step in range(SLICES + 4):
+            for stage, lag in order:
+                if 0 <= step - lag < SLICES:
+                    stage(step - lag)
+            if step == 2:
+                quantize_w2(1)
+            if step == PACK + 4:
+                quantize_a3(0)
+        quantize_a3(1)
+
+        tiles = N // P
+        accs = [psum.tile([P, tiles, P3 // 2], F32, name="acc", bufs=4) for u in range(2)]
         for b in range(PASSES):
             for u in range(2):
-                for e in range(2):
-                    cols = slice((2 * u + e) * P, (2 * u + e + 1) * P)
+                for e in range(tiles):
+                    cols = slice(e * P, (e + 1) * P)
                     nc.tensor.matmul_mx(
                         out=accs[u][:, e, :],
                         lhsT=w2_c[:, b, cols].bitcast(FP8X4),
                         lhsT_scale=w2_s[:, b, cols],
-                        rhs=a3_c[b][:].bitcast(FP8X4),
-                        rhs_scale=a3_s[b][:],
+                        rhs=a3_c[b][u][:].bitcast(FP8X4),
+                        rhs_scale=a3_s[b][u][:],
                         start=(b == 0 and e == 0),
-                        stop=(b == PASSES - 1 and e == 1),
+                        stop=(b == PASSES - 1 and e == tiles - 1),
                     )
-        for u in range(2):
-            res = work.tile([P, 2, P3], F32, name="res")
+        for u, (cols, entries) in enumerate(halves(P3)):
+            res = work.tile([P, tiles, P3 // 2], F32, name="res")
             nc.scalar.activation(out=res[:], in_=accs[u][:], func=ACT.Tanh)
-            nc.sync.dma_start(out=halves[u], in_=res[:])
+            nc.sync.dma_start(out=out[:, cols].rearrange("(e p) j -> p e j", p=P), in_=res[:])

@@ -23,7 +23,7 @@ K_PASS = P * PACK
 PASSES = H // K_PASS
 SLICES = H // P
 BANK = 512
-MOVED = 512
+MOVED = 768
 
 
 def load_scale_rows(queue, plane, rows):
@@ -45,26 +45,35 @@ def tile_list_vegetable_class_judging_kernel(
             nc.sync.dma_start(tile[:], src)
             return tile
 
-        tab_w = keep.tile([P, T], U32, align_bytes=64, tag="tab_w")
+        idx = load_list(offs, "idx")
+        tab_w = keep.tile([P, T], U32, align_bytes=64)
         nc.sync.dma_start(out=tab_w[:].bitcast(I32), in_=tab_words[0].rearrange("p t i -> p (t i)").bitcast(I32))
-        idx, p1, p2, p3 = [load_list(src, name) for src, name in ((offs, "idx"), (pos1, "p1"), (pos2, "p2"), (pos3, "p3"))]
-        p4, p5, p6 = [load_list(src, name) for src, name in ((pos4, "p4"), (pos5, "p5"), (pos6, "p6"))]
+        p1, p2, p3, p4, p5, p6 = [
+            load_list(src, "p%d" % (i + 1)) for i, src in enumerate((pos1, pos2, pos3, pos4, pos5, pos6))
+        ]
+        w2_raw = []
+        for b in range(PASSES):
+            raw = keep.tile([P, PACK, N], F32, name="w2_raw%d" % b)
+            nc.sync.dma_start(out=raw[:], in_=w2[b * K_PASS : (b + 1) * K_PASS, :].rearrange("(p t) n -> p t n", t=PACK))
+            w2_raw.append(raw)
+        d_col = keep.tile([P, P2 // P], F32)
+        with nc.allow_non_contiguous_dma(reason="one value of d for each partition"):
+            nc.sync.dma_start(out=d_col[:], in_=d.rearrange("(c p) -> p c", p=P))
+        gain_col = keep.tile([P, PASSES, PACK], F32)
+        nc.sync.dma_start(out=gain_col[:], in_=gain.rearrange("(b p t) -> p b t", b=PASSES, t=PACK))
+        d_row = keep.tile([P, P2], F32)
+        nc.sync.dma_start(out=d_row[:], in_=d.partition_broadcast(P))
 
-        w4_raw = keep.tile([P, 2 * H], U8, align_bytes=64, tag="w4_raw")
+        w4_raw = keep.tile([P, 2 * H], U8, align_bytes=64)
         nc.gpsimd.dma_start(out=w4_raw[:].bitcast(I32), in_=w4_words[0].bitcast(I32))
         w4s_raw = keep.tile([P, H], U8, align_bytes=64)
         nc.vector.memset(w4s_raw[:].bitcast(I32), 0)
         tab_s = keep.tile([P, T], U8, align_bytes=64, tag="tab_s")
         nc.vector.memset(tab_s[:].bitcast(I32), 0)
-        load_scale_rows(nc.scalar, w4s_raw, w4_scales[0])
+        load_scale_rows(nc.gpsimd, w4s_raw, w4_scales[0])
         load_scale_rows(nc.scalar, tab_s, tab_scales[0])
         ident = keep.tile([P, P], F32)
         make_identity(nc, ident[:])
-        gain_col = keep.tile([P, PASSES, PACK], F32)
-        nc.gpsimd.dma_start(out=gain_col[:], in_=gain.rearrange("(b p t) -> p b t", b=PASSES, t=PACK))
-        d_col = keep.tile([P, P2 // P], F32)
-        with nc.allow_non_contiguous_dma(reason="one value of d for each partition"):
-            nc.gpsimd.dma_start(out=d_col[:], in_=d.rearrange("(c p) -> p c", p=P))
 
         w4_c = keep.tile([P, SLICES, 2 * P], U8, align_bytes=64)
         nc.vector.tensor_copy(
@@ -89,14 +98,7 @@ def tile_list_vegetable_class_judging_kernel(
             nc.vector.tensor_copy(scales[:], tab_s[:].indirect(idx[:, c * BANK // 16 : (c + 1) * BANK // 16]))
             v_s.append(scales)
 
-        w2_raw = []
-        for b, tag in enumerate(("w4_raw", "tab_w")):
-            raw = keep.tile([P, PACK, N], F32, align_bytes=64, name="w2_raw%d" % b, tag=tag)
-            nc.sync.dma_start(out=raw[:], in_=w2[b * K_PASS : (b + 1) * K_PASS, :].rearrange("(p t) n -> p t n", t=PACK))
-            w2_raw.append(raw)
-        d_row = keep.tile([P, P2], F32, align_bytes=64, tag="tab_s")
-        nc.sync.dma_start(out=d_row[:], in_=d.partition_broadcast(P))
-        w2_c = keep.tile([P, PASSES, N], U32, align_bytes=64)
+        w2_c = keep.tile([P, PASSES, N], U32, align_bytes=64, tag="tab_s")
         w2_s = keep.tile([P, PASSES, N], U8, align_bytes=64)
 
         def quantize_w2(b):
@@ -120,27 +122,33 @@ def tile_list_vegetable_class_judging_kernel(
         a3_s = per_half([P, P3 // 2], U8, "a3_s")
         h, a1, a2 = {}, {}, {}
 
-        def features(s):
-            h[s] = work.tile([P, S], F32, name="h", bufs=2)
-            for c in range(S // BANK):
-                cols = slice(c * BANK, (c + 1) * BANK)
-                acc = psum.tile([P, BANK], F32, name="acc", bufs=4)
-                nc.tensor.matmul_mx(
-                    out=acc[:],
-                    lhsT=w4_c[:, s, :].bitcast(FP4X4),
-                    lhsT_scale=w4_s[:, s, :],
-                    rhs=v_w[c][:].bitcast(FP8X4),
-                    rhs_scale=v_s[c][:],
-                    start=True,
-                    stop=True,
-                )
-                nc.scalar.activation(out=h[s][:, cols], in_=acc[:], func=ACT.Silu)
+        banks = [psum.tile([P, BANK], F32, name="bank%d" % i, bufs=1) for i in range(4)]
 
-        def turned(terms, name):
-            bank = psum.tile([P, BANK], F32, name=name)
-            count = BANK // P * len(terms)
+        def next_bank():
+            banks.append(banks.pop(0))
+            return banks[-1]
+
+        def features(s, c):
+            if c == 0:
+                h[s] = work.tile([P, S], F32, name="h", bufs=2)
+            bank = next_bank()
+            nc.tensor.matmul_mx(
+                out=bank[:],
+                lhsT=w4_c[:, s, :].bitcast(FP4X4),
+                lhsT_scale=w4_s[:, s, :],
+                rhs=v_w[c][:].bitcast(FP8X4),
+                rhs_scale=v_s[c][:],
+                start=True,
+                stop=True,
+            )
+            nc.scalar.activation(out=h[s][:, c * BANK : (c + 1) * BANK], in_=bank[:], func=ACT.Silu)
+
+        def turned(terms):
+            width = terms[0].shape[1]
+            bank = next_bank()[:, :width]
+            count = width // P * len(terms)
             n = 0
-            for blk in range(BANK // P):
+            for blk in range(width // P):
                 cols = slice(blk * P, (blk + 1) * P)
                 for term in terms:
                     nc.tensor.matmul(
@@ -156,49 +164,65 @@ def tile_list_vegetable_class_judging_kernel(
             half = width // 2
             return [(slice(u * half, (u + 1) * half), slice(u * half // 16, (u + 1) * half // 16)) for u in range(2)]
 
-        (moved, moved_entries), (kept, kept_entries) = halves(P1)
+        moved, moved_entries = slice(0, MOVED), slice(0, MOVED // 16)
+        kept, kept_entries = slice(MOVED, P1), slice(MOVED // 16, P1 // 16)
 
-        veg, other = {}, {}
+        pending, prods, diffs, other = {}, {}, {}, {}
 
         def level1(s):
             window = h[s][:]
             a1[s] = work.tile([P, P1], F32, name="a1", bufs=4)
             first = work.tile([P, P1], F32, name="first", bufs=3)
             nc.vector.tensor_copy(first[:], window.indirect(p1[:]))
-            nc.vector.tensor_copy(scratch[:], window.indirect(p2[:, kept_entries]))
-            gap = work.tile([P, BANK], F32, name="gap", bufs=3)
+            second = scratch[:, : P1 - MOVED]
+            nc.vector.tensor_copy(second, window.indirect(p2[:, kept_entries]))
+            gap = work.tile([P, MOVED], F32, name="gap", bufs=3)
             nc.vector.tensor_tensor(gap[:], window.indirect(p2[:, moved_entries]), first[:, moved], ALU.subtract)
-            nc.vector.tensor_tensor(a1[s][:, kept], first[:, kept], scratch[:], ALU.max)
-            rise = work.tile([P, BANK], F32, name="rise")
-            nc.scalar.activation(out=rise[:], in_=gap[:], func=ACT.Relu)
-            bank = turned([first, rise], "there")
-            across = work.tile([P, BANK], F32, name="across", bufs=3)
-            nc.scalar.copy(out=across[:], in_=bank[:])
-            bank = turned([across], "back")
-            nc.scalar.copy(out=a1[s][:, moved], in_=bank[:])
+            nc.vector.tensor_tensor(a1[s][:, kept], first[:, kept], second, ALU.max)
+            pending[s] = first, gap
+
+        pieces = [slice(c0, min(c0 + BANK, MOVED)) for c0 in range(0, MOVED, BANK)]
+        across = {}
+        rises = keep.tile([P, MOVED], F32)
+
+        def rise(s):
+            nc.scalar.activation(out=rises[:], in_=pending[s][1][:], func=ACT.Relu)
+
+        def larger_across(s, u):
+            cols = pieces[u]
+            bank = turned([pending[s][0][:, cols], rises[:, cols]])
+            across[s, u] = rises[:, cols]
+            nc.scalar.copy(out=across[s, u], in_=bank)
+
+        def larger_back(s, u):
+            nc.scalar.copy(out=a1[s][:, pieces[u]], in_=turned([across[s, u]]))
 
         def first_vegs(s):
             nc.vector.tensor_copy(scratch[:], a1[s][:].indirect(p3[:]))
 
         def products(s):
-            prod = work.tile([P, P2], F32, name="prod")
-            nc.vector.tensor_tensor(prod[:], a1[s][:].indirect(p4[:]), scratch[:], ALU.mult)
+            prods[s] = work.tile([P, P2], F32, name="prod")
+            nc.vector.tensor_tensor(prods[s][:], a1[s][:].indirect(p4[:]), scratch[:], ALU.mult)
+
+        def offset_across(s):
             a2[s] = work.tile([P, P2], F32, name="a2", bufs=4)
             if s == last:
-                nc.vector.tensor_tensor(a2[s][:], prod[:], d_row[:], ALU.add)
+                nc.vector.tensor_tensor(a2[s][:], prods[s][:], d_row[:], ALU.add)
                 return
-            bank = turned([prod], "there")
-            across = work.tile([P, BANK], F32, name="across", bufs=3)
+            bank = turned([prods[s][:]])
+            across[s, "d"] = work.tile([P, BANK], F32, name="across", bufs=4)
             for blk in range(P2 // P):
                 cols = slice(blk * P, (blk + 1) * P)
                 nc.scalar.activation(
-                    out=across[:, cols], in_=bank[:, cols], func=ACT.Identity, bias=d_col[:, blk : blk + 1]
+                    out=across[s, "d"][:, cols], in_=bank[:, cols], func=ACT.Identity, bias=d_col[:, blk : blk + 1]
                 )
-            bank = turned([across], "back")
-            nc.scalar.copy(out=a2[s][:], in_=bank[:])
+
+        def offset_back(s):
+            if s != last:
+                nc.scalar.copy(out=a2[s][:], in_=turned([across[s, "d"][:]]))
 
         def second_growers(s):
-            other[s] = h[min(s + 4, last)][:, :P3]
+            other[s] = h[min(s + 4, last)][:, s * P3 : (s + 1) * P3]
             nc.vector.tensor_copy(other[s], a2[s][:].indirect(p6[:]))
 
         def differences(s):
@@ -207,6 +231,11 @@ def tile_list_vegetable_class_judging_kernel(
             diff = work.tile([P, P3], F32, name="diff", bufs=3)
             for cols, entries in parts:
                 nc.vector.tensor_tensor(diff[:, cols], a2[s][:].indirect(p5[:, entries]), other[s][:, cols], ALU.subtract)
+            diffs[s] = diff
+
+        def rounded(s):
+            b, t = divmod(s, PACK)
+            diff = diffs[s]
             for u, (cols, entries) in enumerate(halves(P3)):
                 nc.scalar.activation(
                     out=a3_bf[b][u][:, :, t], in_=diff[:, cols], func=ACT.Copy, scale=gain_col[:, b, t : t + 1]
@@ -220,27 +249,31 @@ def tile_list_vegetable_class_judging_kernel(
                     in_=a3_bf[b][u][:].rearrange("p j t -> p (j t)"),
                 )
 
-        features(0)
-        quantize_w2(0)
-        order = ((features, -1), (level1, 0), (second_growers, 4), (first_vegs, 2), (differences, 4), (products, 2))
-        for step in range(SLICES + 4):
-            for stage, lag in order:
+        for c in range(S // BANK):
+            features(0, c)
+        for b in range(PASSES):
+            quantize_w2(b)
+        order = (
+            (level1, 0), (second_growers, 4), (first_vegs, 2), (differences, 4), (products, 2),
+            (rise, 1), (features, -1, 0), (larger_across, 1, 0), (offset_across, 3), (features, -1, 1), (larger_across, 1, 1),
+            (offset_back, 3), (features, -1, 2), (larger_back, 1, 0), (larger_back, 1, 1), (rounded, 5), (features, -1, 3),
+        )
+        for step in range(SLICES + 5):
+            for stage, lag, *part in sorted(order, key=lambda entry: not (step == 1 and entry[0] is features)):
                 if 0 <= step - lag < SLICES:
-                    stage(step - lag)
-            if step == 2:
-                quantize_w2(1)
-            if step == PACK + 4:
+                    stage(step - lag, *part)
+            if step == PACK + 5:
                 quantize_a3(0)
         quantize_a3(1)
 
         tiles = N // P
-        accs = [psum.tile([P, tiles, P3 // 2], F32, name="acc", bufs=4) for u in range(2)]
+        accs = [next_bank() for u in range(2)]
         for b in range(PASSES):
             for u in range(2):
                 for e in range(tiles):
                     cols = slice(e * P, (e + 1) * P)
                     nc.tensor.matmul_mx(
-                        out=accs[u][:, e, :],
+                        out=accs[u][:, cols],
                         lhsT=w2_c[:, b, cols].bitcast(FP8X4),
                         lhsT_scale=w2_s[:, b, cols],
                         rhs=a3_c[b][u][:].bitcast(FP8X4),
@@ -250,5 +283,5 @@ def tile_list_vegetable_class_judging_kernel(
                     )
         for u, (cols, entries) in enumerate(halves(P3)):
             res = work.tile([P, tiles, P3 // 2], F32, name="res")
-            nc.scalar.activation(out=res[:], in_=accs[u][:], func=ACT.Tanh)
+            nc.scalar.activation(out=res[:].rearrange("p e j -> p (e j)"), in_=accs[u][:], func=ACT.Tanh)
             nc.sync.dma_start(out=out[:, cols].rearrange("(e p) j -> p e j", p=P), in_=res[:])

@@ -1,7 +1,6 @@
 from contextlib import ExitStack
 
 import concourse.mybir as mybir
-from concourse.masks import make_identity
 
 K, H, N, T, S, P1, P2, P3 = 512, 1024, 512, 4096, 2048, 1024, 512, 256
 FLOPS = 2 * K * H * S + 2 * H * N * P3
@@ -45,67 +44,66 @@ def tile_list_vegetable_class_judging_kernel(
             nc.sync.dma_start(tile[:], src)
             return tile
 
-        idx = load_list(offs, "idx")
-        tab_w = keep.tile([P, T], U32, align_bytes=64)
-        nc.sync.dma_start(out=tab_w[:].bitcast(I32), in_=tab_words[0].rearrange("p t i -> p (t i)").bitcast(I32))
-        p1, p2, p3, p4, p5, p6 = [
-            load_list(src, "p%d" % (i + 1)) for i, src in enumerate((pos1, pos2, pos3, pos4, pos5, pos6))
+        idx, p1, p2, p3, p4, p5, p6 = [
+            load_list(src, "list%d" % i) for i, src in enumerate((offs, pos1, pos2, pos3, pos4, pos5, pos6))
         ]
-        w2_raw = []
-        for b in range(PASSES):
-            raw = keep.tile([P, PACK, N], F32, name="w2_raw%d" % b)
-            nc.sync.dma_start(out=raw[:], in_=w2[b * K_PASS : (b + 1) * K_PASS, :].rearrange("(p t) n -> p t n", t=PACK))
-            w2_raw.append(raw)
-        d_col = keep.tile([P, P2 // P], F32)
-        with nc.allow_non_contiguous_dma(reason="one value of d for each partition"):
-            nc.sync.dma_start(out=d_col[:], in_=d.rearrange("(c p) -> p c", p=P))
-        gain_col = keep.tile([P, PASSES, PACK], F32)
-        nc.sync.dma_start(out=gain_col[:], in_=gain.rearrange("(b p t) -> p b t", b=PASSES, t=PACK))
-        d_row = keep.tile([P, P2], F32)
-        nc.sync.dma_start(out=d_row[:], in_=d.partition_broadcast(P))
-
-        w4_raw = keep.tile([P, 2 * H], U8, align_bytes=64)
-        nc.gpsimd.dma_start(out=w4_raw[:].bitcast(I32), in_=w4_words[0].bitcast(I32))
-        w4s_raw = keep.tile([P, H], U8, align_bytes=64)
-        nc.vector.memset(w4s_raw[:].bitcast(I32), 0)
+        w4_raw = keep.tile([P, 2 * H], U8, align_bytes=64, tag="w4")
+        nc.sync.dma_start(out=w4_raw[:].bitcast(I32), in_=w4_words[0].bitcast(I32))
         tab_s = keep.tile([P, T], U8, align_bytes=64, tag="tab_s")
         nc.vector.memset(tab_s[:].bitcast(I32), 0)
-        load_scale_rows(nc.gpsimd, w4s_raw, w4_scales[0])
-        load_scale_rows(nc.scalar, tab_s, tab_scales[0])
+        load_scale_rows(nc.sync, tab_s, tab_scales[0])
+        zeros = keep.tile([P, P], F32, align_bytes=64, tag="tab_w")
+        nc.vector.memset(zeros[:], 0.0)
         ident = keep.tile([P, P], F32)
-        make_identity(nc, ident[:])
+        nc.gpsimd.affine_select(
+            out=ident[:], in_=zeros[:], compare_op=ALU.not_equal, fill=1.0, base=0, pattern=[[-1, P]], channel_multiplier=1
+        )
+        tab_w = keep.tile([P, T], U32, align_bytes=64, tag="tab_w")
+        nc.sync.dma_start(out=tab_w[:].bitcast(I32), in_=tab_words[0].rearrange("p t i -> p (t i)").bitcast(I32))
 
         w4_c = keep.tile([P, SLICES, 2 * P], U8, align_bytes=64)
         nc.vector.tensor_copy(
             out=w4_c[:].bitcast(U16).rearrange("p (b t) m -> p b t m", t=PACK),
             in_=w4_raw[:].bitcast(U16).rearrange("p (b m t) -> p b t m", b=PASSES, t=PACK),
         )
+        w4s_raw = keep.tile([P, H], U8, align_bytes=64, tag="w4")
+        nc.vector.memset(w4s_raw[:].bitcast(I32), 0)
+        load_scale_rows(nc.sync, w4s_raw, w4_scales[0])
+        v_s = keep.tile([P, S], U8, align_bytes=64)
+        nc.vector.tensor_copy(v_s[:], tab_s[:].indirect(idx[:]))
         w4_s = keep.tile([P, SLICES, P], U8, align_bytes=64)
         nc.vector.tensor_copy(
             out=w4_s[:].rearrange("p (b t) m -> p b t m", t=PACK),
             in_=w4s_raw[:].rearrange("p (b m t) -> p b t m", b=PASSES, t=PACK),
         )
+        v_first = keep.tile([P, BANK], U32, align_bytes=64)
+        v_rest = keep.tile([P, S - BANK], U32, align_bytes=64, tag="w4")
+        v_w = [v_first[:]] + [v_rest[:, c0 : c0 + BANK] for c0 in range(0, S - BANK, BANK)]
+        for c, words in enumerate(v_w):
+            nc.vector.tensor_copy(words, tab_w[:].indirect(idx[:, c * BANK // 16 : (c + 1) * BANK // 16]))
 
-        v_w = []
-        for c in range(S // BANK):
-            words = keep.tile([P, BANK], U32, align_bytes=64, name="v_w%d" % c)
-            nc.vector.tensor_copy(words[:], tab_w[:].indirect(idx[:, c * BANK // 16 : (c + 1) * BANK // 16]))
-            v_w.append(words)
-
-        v_s = []
-        for c in range(S // BANK):
-            scales = keep.tile([P, BANK], U8, align_bytes=64, name="v_s%d" % c)
-            nc.vector.tensor_copy(scales[:], tab_s[:].indirect(idx[:, c * BANK // 16 : (c + 1) * BANK // 16]))
-            v_s.append(scales)
-
-        w2_c = keep.tile([P, PASSES, N], U32, align_bytes=64, tag="tab_s")
+        late = keep.tile([P, T], F32, align_bytes=64, tag="tab_w")
+        w2_raw = []
+        for b in range(PASSES):
+            raw = late[:, b * PACK * N : (b + 1) * PACK * N].rearrange("p (t n) -> p t n", t=PACK)
+            nc.sync.dma_start(out=raw, in_=w2[b * K_PASS : (b + 1) * K_PASS, :].rearrange("(p t) n -> p t n", t=PACK))
+            w2_raw.append(raw)
+        small = keep.tile([P, P2 + 16], F32, align_bytes=64, tag="tab_s")
+        d_col = small[:, P2 : P2 + 4]
+        with nc.allow_non_contiguous_dma(reason="one value of d for each partition"):
+            nc.sync.dma_start(out=d_col, in_=d.rearrange("(c p) -> p c", p=P))
+        gain_col = small[:, P2 + 8 : P2 + 16].rearrange("p (b t) -> p b t", t=PACK)
+        nc.sync.dma_start(out=gain_col, in_=gain.rearrange("(b p t) -> p b t", b=PASSES, t=PACK))
+        d_row = small[:, :P2]
+        nc.sync.dma_start(out=d_row, in_=d.partition_broadcast(P))
+        w2_c = keep.tile([P, PASSES, N], U32, align_bytes=64)
         w2_s = keep.tile([P, PASSES, N], U8, align_bytes=64)
 
         def quantize_w2(b):
             grouped = keep.tile([P, N, PACK], BF16, align_bytes=64, name="w2_bf%d" % b)
             nc.scalar.copy(
                 out=grouped[:].rearrange("p (c i) t -> p c t i", i=4),
-                in_=w2_raw[b][:].rearrange("p t (c i) -> p c t i", i=4),
+                in_=w2_raw[b].rearrange("p t (c i) -> p c t i", i=4),
             )
             nc.vector.quantize_mx(
                 out=w2_c[:, b, :].bitcast(FP8X4), scales=w2_s[:, b, :], in_=grouped[:].rearrange("p n t -> p (n t)")
@@ -136,8 +134,8 @@ def tile_list_vegetable_class_judging_kernel(
                 out=bank[:],
                 lhsT=w4_c[:, s, :].bitcast(FP4X4),
                 lhsT_scale=w4_s[:, s, :],
-                rhs=v_w[c][:].bitcast(FP8X4),
-                rhs_scale=v_s[c][:],
+                rhs=v_w[c].bitcast(FP8X4),
+                rhs_scale=v_s[:, c * BANK : (c + 1) * BANK],
                 start=True,
                 stop=True,
             )
@@ -207,7 +205,7 @@ def tile_list_vegetable_class_judging_kernel(
         def offset_across(s):
             a2[s] = work.tile([P, P2], F32, name="a2", bufs=4)
             if s == last:
-                nc.vector.tensor_tensor(a2[s][:], prods[s][:], d_row[:], ALU.add)
+                nc.vector.tensor_tensor(a2[s][:], prods[s][:], d_row, ALU.add)
                 return
             bank = turned([prods[s][:]])
             across[s, "d"] = work.tile([P, BANK], F32, name="across", bufs=4)
@@ -251,8 +249,6 @@ def tile_list_vegetable_class_judging_kernel(
 
         for c in range(S // BANK):
             features(0, c)
-        for b in range(PASSES):
-            quantize_w2(b)
         order = (
             (level1, 0), (second_growers, 4), (first_vegs, 2), (differences, 4), (products, 2),
             (rise, 1), (features, -1, 0), (larger_across, 1, 0), (offset_across, 3), (features, -1, 1), (larger_across, 1, 1),
@@ -262,6 +258,8 @@ def tile_list_vegetable_class_judging_kernel(
             for stage, lag, *part in sorted(order, key=lambda entry: not (step == 1 and entry[0] is features)):
                 if 0 <= step - lag < SLICES:
                     stage(step - lag, *part)
+            if step in (0, 4):
+                quantize_w2((0, 4).index(step))
             if step == PACK + 5:
                 quantize_a3(0)
         quantize_a3(1)

from contextlib import ExitStack

import concourse.mybir as mybir

K, H, N, T, S, P1, P2, P3 = 512, 1024, 512, 4096, 2048, 1024, 512, 256
FLOPS = 2 * K * H * S + 2 * H * N * P3

F32 = mybir.dt.float32
BF16 = mybir.dt.bfloat16
I32 = mybir.dt.int32
U32 = mybir.dt.uint32
U16 = mybir.dt.uint16
U8 = mybir.dt.uint8
FP8X4 = mybir.dt.float8_e4m3fn_x4
FP4X4 = mybir.dt.float4_e2m1fn_x4
ALU = mybir.AluOpType
ACT = mybir.ActivationFunctionType

P = 128
PACK = 4
K_PASS = P * PACK
PASSES = H // K_PASS
SLICES = H // P
BANK = 512
MOVED = 768


def load_scale_rows(queue, plane, rows):
    for q in range(4):
        queue.dma_start(out=plane[32 * q : 32 * q + 4, :].bitcast(I32), in_=rows[4 * q : 4 * q + 4, :].bitcast(I32))


def tile_list_vegetable_class_judging_kernel(
    tc, tab_words, tab_scales, offs, pos1, pos2, pos3, pos4, pos5, pos6, w4_words, w4_scales, d, gain, w2, out
):
    nc = tc.nc
    with ExitStack() as ctx:
        keep = ctx.enter_context(tc.tile_pool(name="keep", bufs=1))
        work = ctx.enter_context(tc.tile_pool(name="work", bufs=2))
        psum = ctx.enter_context(tc.psum_pool(name="psum", bufs=2))

        def load_list(src, name):
            tile = keep.tile(list(src.shape), U16, name=name)
            nc.sync.dma_start(tile[:], src)
            return tile

        idx, p1, p2, p3, p4, p5, p6 = [
            load_list(src, "list%d" % i) for i, src in enumerate((offs, pos1, pos2, pos3, pos4, pos5, pos6))
        ]
        w4_raw = keep.tile([P, 2 * H], U8, align_bytes=64, tag="w4")
        nc.sync.dma_start(out=w4_raw[:].bitcast(I32), in_=w4_words[0].bitcast(I32))
        tab_s = keep.tile([P, T], U8, align_bytes=64, tag="tab_s")
        nc.vector.memset(tab_s[:].bitcast(I32), 0)
        load_scale_rows(nc.sync, tab_s, tab_scales[0])
        zeros = keep.tile([P, P], F32, align_bytes=64, tag="tab_w")
        nc.vector.memset(zeros[:], 0.0)
        ident = keep.tile([P, P], F32)
        nc.gpsimd.affine_select(
            out=ident[:], in_=zeros[:], compare_op=ALU.not_equal, fill=1.0, base=0, pattern=[[-1, P]], channel_multiplier=1
        )
        tab_w = keep.tile([P, T], U32, align_bytes=64, tag="tab_w")
        nc.sync.dma_start(out=tab_w[:].bitcast(I32), in_=tab_words[0].rearrange("p t i -> p (t i)").bitcast(I32))

        w4_c = keep.tile([P, SLICES, 2 * P], U8, align_bytes=64)
        nc.vector.tensor_copy(
            out=w4_c[:].bitcast(U16).rearrange("p (b t) m -> p b t m", t=PACK),
            in_=w4_raw[:].bitcast(U16).rearrange("p (b m t) -> p b t m", b=PASSES, t=PACK),
        )
        w4s_raw = keep.tile([P, H], U8, align_bytes=64, tag="w4")
        nc.vector.memset(w4s_raw[:].bitcast(I32), 0)
        load_scale_rows(nc.sync, w4s_raw, w4_scales[0])
        v_s = keep.tile([P, S], U8, align_bytes=64)
        nc.vector.tensor_copy(v_s[:], tab_s[:].indirect(idx[:]))
        w4_s = keep.tile([P, SLICES, P], U8, align_bytes=64)
        nc.vector.tensor_copy(
            out=w4_s[:].rearrange("p (b t) m -> p b t m", t=PACK),
            in_=w4s_raw[:].rearrange("p (b m t) -> p b t m", b=PASSES, t=PACK),
        )
        v_first = keep.tile([P, BANK], U32, align_bytes=64)
        v_rest = keep.tile([P, S - BANK], U32, align_bytes=64, tag="w4")
        v_w = [v_first[:]] + [v_rest[:, c0 : c0 + BANK] for c0 in range(0, S - BANK, BANK)]
        for c, words in enumerate(v_w):
            nc.vector.tensor_copy(words, tab_w[:].indirect(idx[:, c * BANK // 16 : (c + 1) * BANK // 16]))

        late = keep.tile([P, T], F32, align_bytes=64, tag="tab_w")
        w2_raw = []
        for b in range(PASSES):
            raw = late[:, b * PACK * N : (b + 1) * PACK * N].rearrange("p (t n) -> p t n", t=PACK)
            nc.sync.dma_start(out=raw, in_=w2[b * K_PASS : (b + 1) * K_PASS, :].rearrange("(p t) n -> p t n", t=PACK))
            w2_raw.append(raw)
        small = keep.tile([P, P2 + 16], F32, align_bytes=64, tag="tab_s")
        d_col = small[:, P2 : P2 + 4]
        with nc.allow_non_contiguous_dma(reason="one value of d for each partition"):
            nc.sync.dma_start(out=d_col, in_=d.rearrange("(c p) -> p c", p=P))
        gain_col = small[:, P2 + 8 : P2 + 16].rearrange("p (b t) -> p b t", t=PACK)
        nc.sync.dma_start(out=gain_col, in_=gain.rearrange("(b p t) -> p b t", b=PASSES, t=PACK))
        d_row = small[:, :P2]
        nc.sync.dma_start(out=d_row, in_=d.partition_broadcast(P))
        w2_c = keep.tile([P, PASSES, N], U32, align_bytes=64)
        w2_s = keep.tile([P, PASSES, N], U8, align_bytes=64)

        def quantize_w2(b):
            grouped = keep.tile([P, N, PACK], BF16, align_bytes=64, name="w2_bf%d" % b)
            nc.scalar.copy(
                out=grouped[:].rearrange("p (c i) t -> p c t i", i=4),
                in_=w2_raw[b].rearrange("p t (c i) -> p c t i", i=4),
            )
            nc.vector.quantize_mx(
                out=w2_c[:, b, :].bitcast(FP8X4), scales=w2_s[:, b, :], in_=grouped[:].rearrange("p n t -> p (n t)")
            )

        def per_half(shape, dtype, name):
            return [
                [keep.tile(shape, dtype, align_bytes=64, name="%s%d%d" % (name, b, u)) for u in range(2)]
                for b in range(PASSES)
            ]

        a3_bf = per_half([P, P3 // 2, PACK], BF16, "a3_bf")
        a3_c = per_half([P, P3 // 2], U32, "a3_c")
        a3_s = per_half([P, P3 // 2], U8, "a3_s")
        h, a1, a2 = {}, {}, {}

        banks = [psum.tile([P, BANK], F32, name="bank%d" % i, bufs=1) for i in range(4)]

        def next_bank():
            banks.append(banks.pop(0))
            return banks[-1]

        def features(s, c):
            if c == 0:
                h[s] = work.tile([P, S], F32, name="h", bufs=2)
            bank = next_bank()
            nc.tensor.matmul_mx(
                out=bank[:],
                lhsT=w4_c[:, s, :].bitcast(FP4X4),
                lhsT_scale=w4_s[:, s, :],
                rhs=v_w[c].bitcast(FP8X4),
                rhs_scale=v_s[:, c * BANK : (c + 1) * BANK],
                start=True,
                stop=True,
            )
            nc.scalar.activation(out=h[s][:, c * BANK : (c + 1) * BANK], in_=bank[:], func=ACT.Silu)

        def turned(terms):
            width = terms[0].shape[1]
            bank = next_bank()[:, :width]
            count = width // P * len(terms)
            n = 0
            for blk in range(width // P):
                cols = slice(blk * P, (blk + 1) * P)
                for term in terms:
                    nc.tensor.matmul(
                        bank[:, cols], term[:, cols], ident[:], is_transpose=True, start=(n == 0), stop=(n == count - 1)
                    )
                    n += 1
            return bank

        scratch = keep.tile([P, BANK], F32)
        last = SLICES - 1

        def halves(width):
            half = width // 2
            return [(slice(u * half, (u + 1) * half), slice(u * half // 16, (u + 1) * half // 16)) for u in range(2)]

        moved, moved_entries = slice(0, MOVED), slice(0, MOVED // 16)
        kept, kept_entries = slice(MOVED, P1), slice(MOVED // 16, P1 // 16)

        pending, prods, diffs, other = {}, {}, {}, {}

        def level1(s):
            window = h[s][:]
            a1[s] = work.tile([P, P1], F32, name="a1", bufs=4)
            first = work.tile([P, P1], F32, name="first", bufs=3)
            nc.vector.tensor_copy(first[:], window.indirect(p1[:]))
            second = scratch[:, : P1 - MOVED]
            nc.vector.tensor_copy(second, window.indirect(p2[:, kept_entries]))
            gap = work.tile([P, MOVED], F32, name="gap", bufs=3)
            nc.vector.tensor_tensor(gap[:], window.indirect(p2[:, moved_entries]), first[:, moved], ALU.subtract)
            nc.vector.tensor_tensor(a1[s][:, kept], first[:, kept], second, ALU.max)
            pending[s] = first, gap

        pieces = [slice(c0, min(c0 + BANK, MOVED)) for c0 in range(0, MOVED, BANK)]
        across = {}
        rises = keep.tile([P, MOVED], F32)

        def rise(s):
            nc.scalar.activation(out=rises[:], in_=pending[s][1][:], func=ACT.Relu)

        def larger_across(s, u):
            cols = pieces[u]
            bank = turned([pending[s][0][:, cols], rises[:, cols]])
            across[s, u] = rises[:, cols]
            nc.scalar.copy(out=across[s, u], in_=bank)

        def larger_back(s, u):
            nc.scalar.copy(out=a1[s][:, pieces[u]], in_=turned([across[s, u]]))

        def first_vegs(s):
            nc.vector.tensor_copy(scratch[:], a1[s][:].indirect(p3[:]))

        def products(s):
            prods[s] = work.tile([P, P2], F32, name="prod")
            nc.vector.tensor_tensor(prods[s][:], a1[s][:].indirect(p4[:]), scratch[:], ALU.mult)

        def offset_across(s):
            a2[s] = work.tile([P, P2], F32, name="a2", bufs=4)
            if s == last:
                nc.vector.tensor_tensor(a2[s][:], prods[s][:], d_row, ALU.add)
                return
            bank = turned([prods[s][:]])
            across[s, "d"] = work.tile([P, BANK], F32, name="across", bufs=4)
            for blk in range(P2 // P):
                cols = slice(blk * P, (blk + 1) * P)
                nc.scalar.activation(
                    out=across[s, "d"][:, cols], in_=bank[:, cols], func=ACT.Identity, bias=d_col[:, blk : blk + 1]
                )

        def offset_back(s):
            if s != last:
                nc.scalar.copy(out=a2[s][:], in_=turned([across[s, "d"][:]]))

        def second_growers(s):
            other[s] = h[min(s + 4, last)][:, s * P3 : (s + 1) * P3]
            nc.vector.tensor_copy(other[s], a2[s][:].indirect(p6[:]))

        def differences(s):
            b, t = divmod(s, PACK)
            parts = halves(P3) if s == last else [(slice(0, P3), slice(0, P3 // 16))]
            diff = work.tile([P, P3], F32, name="diff", bufs=3)
            for cols, entries in parts:
                nc.vector.tensor_tensor(diff[:, cols], a2[s][:].indirect(p5[:, entries]), other[s][:, cols], ALU.subtract)
            diffs[s] = diff

        def rounded(s):
            b, t = divmod(s, PACK)
            diff = diffs[s]
            for u, (cols, entries) in enumerate(halves(P3)):
                nc.scalar.activation(
                    out=a3_bf[b][u][:, :, t], in_=diff[:, cols], func=ACT.Copy, scale=gain_col[:, b, t : t + 1]
                )

        def quantize_a3(b):
            for u in range(2):
                nc.vector.quantize_mx(
                    out=a3_c[b][u][:].bitcast(FP8X4),
                    scales=a3_s[b][u][:],
                    in_=a3_bf[b][u][:].rearrange("p j t -> p (j t)"),
                )

        for c in range(S // BANK):
            features(0, c)
        order = (
            (level1, 0), (second_growers, 4), (first_vegs, 2), (differences, 4), (products, 2),
            (rise, 1), (features, -1, 0), (larger_across, 1, 0), (offset_across, 3), (features, -1, 1), (larger_across, 1, 1),
            (offset_back, 3), (features, -1, 2), (larger_back, 1, 0), (larger_back, 1, 1), (rounded, 5), (features, -1, 3),
        )
        for step in range(SLICES + 5):
            for stage, lag, *part in sorted(order, key=lambda entry: not (step == 1 and entry[0] is features)):
                if 0 <= step - lag < SLICES:
                    stage(step - lag, *part)
            if step in (0, 4):
                quantize_w2((0, 4).index(step))
            if step == PACK + 5:
                quantize_a3(0)
        quantize_a3(1)

        tiles = N // P
        accs = [next_bank() for u in range(2)]
        for b in range(PASSES):
            for u in range(2):
                for e in range(tiles):
                    cols = slice(e * P, (e + 1) * P)
                    nc.tensor.matmul_mx(
                        out=accs[u][:, cols],
                        lhsT=w2_c[:, b, cols].bitcast(FP8X4),
                        lhsT_scale=w2_s[:, b, cols],
                        rhs=a3_c[b][u][:].bitcast(FP8X4),
                        rhs_scale=a3_s[b][u][:],
                        start=(b == 0 and e == 0),
                        stop=(b == PASSES - 1 and e == tiles - 1),
                    )
        for u, (cols, entries) in enumerate(halves(P3)):
            res = work.tile([P, tiles, P3 // 2], F32, name="res")
            nc.scalar.activation(out=res[:].rearrange("p e j -> p (e j)"), in_=accs[u][:], func=ACT.Tanh)
            nc.sync.dma_start(out=out[:, cols].rearrange("(e p) j -> p e j", p=P), in_=res[:])
